import numpy as np, ml_dtypes
CORES = [1,129,9,137,57,185,105,233,113,241,121,249]
N = 12
import mx_ref
NC, G = 128, 4
EPS = 0.001
BF = ml_dtypes.bfloat16
def cut(t, i, w=512):
    return t[:, w * i:w * i + w]
def tile(rs):
    return np.stack(rs, axis=2).reshape(128, -1).astype(BF)
def layer(w, X):
    out = []
    for i in range(G):
        for t in range(len(X)):
            p = mx_ref.matmul(mx_ref.quantize(cut(w, len(X) * i + t)), X[t])
            z = p if t == 0 else z + p
        out.append(z)
    return out
def normed(Z, s):
    return [z * f for z, f in zip(Z, s)]
def setup_inputs(rng):
    def f(*shape):
        return mx_ref.flush((rng.standard_normal(shape, dtype=np.float32) * np.exp2(rng.integers(-2, 3, shape[:-1] + (1,)))).astype(BF))
    return {"x": f(N, 128, 4 * NC), "w1": f(N, 128, G * 512), "w2": f(N, 128, 512)}
def setup_inputs_blocks(rng):
    d = setup_inputs(rng)
    for k in ("x", "w1", "w2"): d[k] = mx_ref.spread(d[k], rng, 4)
    return d
def setup_inputs_wide(rng):
    d = setup_inputs(rng)
    for k in ("x", "w1", "w2"): d[k] = mx_ref.flush((d[k].astype(np.float32) * np.exp2(rng.integers(-5, 6, (N, 1, 1))).astype(np.float32)).astype(BF))
    return d
def setup_inputs_rows(rng):
    d = setup_inputs(rng); v = d["w1"].astype(np.float32).reshape(N, 128, -1, 4)
    d["w1"] = mx_ref.flush((v * np.exp2(rng.integers(-6, 7, (N, 1, v.shape[2], 1))).astype(np.float32)).reshape(d["w1"].shape).astype(BF))
    return d
def setup_inputs_faint(rng):
    d = setup_inputs(rng); d["x"] = mx_ref.flush((d["x"].astype(np.float32) * np.float32(2.0 ** -12)).astype(BF))
    return d
def reference(x, w1, w2, own=None):
    Z = [layer(w1[r], [mx_ref.quantize(x[r])]) for r in range(N)]
    ms = [sum((Z[r][i].astype(np.float64) ** 2).sum(axis=1, keepdims=True) for r in range(N)) / (N * NC) for i in range(G)]
    s = [(1 / np.sqrt(m + EPS)).astype(np.float32) for m in ms]
    h = np.stack([tile(normed(Z[r], s)) for r in range(N)])
    use = h if own is None else own["h"]
    H = [mx_ref.quantize(use[j]) for j in range(N)]
    y = np.zeros((N, 128, N * NC), np.float32)
    for r in range(N):
        qw = mx_ref.quantize(w2[r])
        for j in range(N):
            y[r][:, NC * j:NC * j + NC] = mx_ref.matmul(qw, H[j])
    return {"h": h, "y": y}

@@ -1,0 +1,216 @@
+from concourse.bass import DstId, RemoteDMATransfer
+from concourse.mybir import dt, AluOpType, AxisListType, ActivationFunctionType
+
+N, NP, NC, G, EPS = 12, 6, 128, 4, 0.001
+NSIM = 256
+TW = 4 * NC
+BANK = 512
+
+SCRATCH = {
+    "xt": ("sbuf", [128, TW], "bfloat16"),
+    "w1t": ("sbuf", [128, G * TW], "bfloat16"),
+    "w2t": ("sbuf", [128, TW], "bfloat16"),
+    "xq": ("sbuf", [128, NC], "float8_e4m3fn_x4"), "xs": ("sbuf", [128, NC], "uint8"),
+    "w1q": ("sbuf", [128, G * NC], "float8_e4m3fn_x4"), "w1s": ("sbuf", [128, G * NC], "uint8"),
+    "w2q": ("sbuf", [128, NC], "float8_e4m3fn_x4"), "w2s": ("sbuf", [128, NC], "uint8"),
+    "ps": ("psum", [128, 8 * BANK], "float32"),
+    "sq": ("sbuf", [128, G * NC], "float32"),
+    "land": ("sbuf", [128, G * N], "float32"),
+    "tot": ("sbuf", [128, G], "float32"), "av": ("sbuf", [128, G], "float32"),
+    "rc": ("sbuf", [128, G], "float32"), "sv": ("sbuf", [128, G], "float32"),
+    "ht": ("sbuf", [128, TW], "bfloat16"),
+    "hq": ("sbuf", [128, N * NC], "float8_e4m3fn_x4"), "hs": ("sbuf", [128, N * NC], "uint8"),
+    "ys": ("sbuf", [128, N * NC], "float32"),
+}
+SEMAPHORES = (["ldx", "ldv", "qx", "qv", "ssd", "ssarr", "red", "va", "vr", "ssq", "hd", "hqd", "st", "sent", "hss", "hcq", "hcs"]
+              + ["ldw%d" % i for i in range(G)] + ["qw%d" % i for i in range(G)] + ["mm%d" % i for i in range(G)]
+              + ["arr%d" % k for k in range(NP)] + ["ym%d" % k for k in range(NP)] + ["yc%d" % k for k in range(NP)])
+
+
+def _bits(mask):
+    return bin(mask).count("1")
+
+
+def _plan(T, topo):
+    cores = list(T.cores)
+    lead = [cores[2 * k] for k in range(NP)]
+    planes = []
+    for k in range(NP):
+        for p in planes:
+            if topo.same_plane(lead[p[0]], lead[k]):
+                p.append(k)
+                break
+        else:
+            planes.append([k])
+    planes.sort(key=len)
+    small, big = planes
+    direct, route = {}, {}
+    for i, k in enumerate(small):
+        direct[k] = small[1 - i]
+        route[k] = [None] * 4
+        for j, o in enumerate(big):
+            route[k][(j + 2 * i) % 4] = (o, j // 2 == i)
+    for j, k in enumerate(big):
+        direct[k] = big[(j + 1) % 4]
+        route[k] = [None] * 4
+        route[k][(j + 3) % 4] = (big[(j + 2) % 4], False)
+        route[k][(j + 2) % 4] = (big[(j + 3) % 4], False)
+        route[k][j % 4] = (small[0], j == 0)
+        route[k][(j + 1) % 4] = (small[1], j == 1)
+    helpers, job = {}, {}
+    for r in range(N):
+        rc, k, a = cores[r], r // 2, r % 2
+        chipc = [c for c in range(NSIM) if c != rc and topo.host(c) == topo.host(rc) and topo.chip(c) == topo.chip(rc)]
+        reach = {c: sum(1 for d in cores if topo.may_write(c, d)) for c in chipc}
+        used, helpers[r] = [], []
+        for o, near in route[k]:
+            dests = [2 * o + a, 2 * o + 1 - a]
+            cand = [c for c in chipc if c not in used and (topo.die(c) == topo.die(rc)) == near
+                    and all(topo.may_write(c, cores[d]) for d in dests)]
+            cand.sort(key=lambda c: (reach[c], c))
+            used.append(cand[0])
+            helpers[r].append((cand[0], dests))
+            job[cand[0]] = (r, dests)
+    order = {}
+    for k in range(NP):
+        order[k] = [k] + [p for p in range(NP) if direct[p] == k]
+        for pos in range(4):
+            order[k] += [p for p in range(NP) if p != k and route[p][pos][0] == k]
+    return {"cores": cores, "direct": direct, "helpers": helpers, "job": job, "order": order}
+
+
+def _send(g, topo, core, view_src, view_dst, dests, mask, rsem, lsem):
+    ids = []
+    for d in dests:
+        rid, pid = topo.addr(d, core)
+        ids.append(DstId(rid=rid, pnc=pid))
+    g.remote_dma_fused([RemoteDMATransfer(dst_ids=ids, dma_engine_mask=mask, remote_sem=rsem,
+                                          srcs=[view_src], dsts=[view_dst] * len(dests))], local_sem=lsem)
+
+
+def _views(T, r):
+    ss = T.land[:, G * r:G * r + G]
+    codes = T.hq[:, NC * r:NC * r + NC].bitcast(dt.uint8)
+    plane = T.hs[:, NC * r:NC * r + NC]
+    return ss, codes, plane
+
+
+def _common(topo, core, dests):
+    m = topo.mask(core, dests[0])
+    for d in dests[1:]:
+        m &= topo.mask(core, d)
+    return m
+
+
+def _helper(g, core, T, topo, P):
+    r, ranks = P["job"][core]
+    S = T.sem
+    dests = [P["cores"][d] for d in ranks]
+    rc = P["cores"][r]
+    on = _common(topo, rc, [h for h, _ in P["helpers"][r]])
+    hi = on & ~_common(topo, rc, [P["cores"][r ^ 1]])
+    m = _common(topo, core, dests)
+    ss, codes, plane = _views(T, r)
+    arr = S["arr%d" % (r // 2)]
+    g.wait_ge(S.hss, _bits(hi))
+    _send(g, topo, core, ss, ss, dests, m, S.ssarr, S.sent)
+    g.wait_ge(S.hcs, _bits(on))
+    _send(g, topo, core, plane, plane, dests, m, arr, S.sent)
+    g.wait_ge(S.hcq, _bits(on))
+    _send(g, topo, core, codes, codes, dests, m, arr, S.sent)
+    g.wait_ge(S.sent, 3 * _bits(m))
+
+
+def _rank(g, core, r, T, topo, P):
+    S, cores = T.sem, P["cores"]
+    k, a = r // 2, r % 2
+    V, A, TE, SY = g.vector, g.scalar, g.tensor, g.sync
+    AF = ActivationFunctionType
+    hcores = [h for h, _ in P["helpers"][r]]
+    o = P["direct"][k]
+    dcores = [cores[r ^ 1], cores[2 * o + a], cores[2 * o + 1 - a]]
+    on = _common(topo, core, hcores)
+    off = _common(topo, core, dcores)
+    hi = on & ~off
+    ss, codes, plane = _views(T, r)
+
+    def bank(b, n):
+        return T.ps[:, BANK * b:BANK * b + n]
+
+    SY.dma_start(T.xt[:], T.x[:]).then_inc(S.ldx, 16)
+    for i in range(G):
+        q = A if i % 2 == 0 else SY
+        q.dma_start(T.w1t[:, TW * i:TW * i + TW], T.w1[:, TW * i:TW * i + TW]).then_inc(S["ldw%d" % i], 16)
+    SY.dma_start(T.w2t[:], T.w2[:]).then_inc(S.ldv, 16)
+    V.wait_ge(S.ldx, 16)
+    V.quantize_mx(T.xq[:], T.xs[:], T.xt[:]).then_inc(S.qx, 1)
+    TE.wait_ge(S.qx, 1)
+    for i in range(G):
+        c0, c1 = NC * i, NC * i + NC
+        V.wait_ge(S["ldw%d" % i], 16)
+        V.quantize_mx(T.w1q[:, c0:c1], T.w1s[:, c0:c1], T.w1t[:, TW * i:TW * i + TW]).then_inc(S["qw%d" % i], 1)
+        TE.wait_ge(S["qw%d" % i], 1)
+        TE.matmul_mx(bank(i, NC), T.w1q[:, c0:c1], T.w1s[:, c0:c1], T.xq[:], T.xs[:], True, True).then_inc(S["mm%d" % i], 1)
+        A.wait_ge(S["mm%d" % i], 1)
+        A.activation(T.sq[:, c0:c1], bank(i, NC), AF.Square,
+                     accum_out=T.land[:, G * r + i:G * r + i + 1]).then_inc(S.ssd, 1)
+    V.wait_ge(S.ldv, 16)
+    V.quantize_mx(T.w2q[:], T.w2s[:], T.w2t[:]).then_inc(S.qv, 1)
+
+    g.wait_ge(S.ssd, G)
+    _send(g, topo, core, ss, ss, hcores, hi, S.hss, S.sent)
+    _send(g, topo, core, ss, ss, dcores, off, S.ssarr, S.sent)
+    V.wait_ge(S.ssd, G)
+    V.wait_ge(S.ssarr, (N - 1) * _bits(off))
+    for i in range(G):
+        V.tensor_reduce(T.tot[:, i:i + 1], T.land[:, i:G * N:G], AxisListType.X, AluOpType.add).then_inc(S.red, 1)
+    V.wait_ge(S.red, G)
+    V.tensor_scalar(T.av[:], T.tot[:], 1.0 / (N * NC), EPS, AluOpType.mult, AluOpType.add).then_inc(S.va, 1)
+    V.wait_ge(S.va, 1)
+    V.reciprocal(T.rc[:], T.av[:]).then_inc(S.vr, 1)
+    A.wait_ge(S.vr, 1)
+    A.activation(T.sv[:], T.rc[:], AF.Sqrt).then_inc(S.ssq, 1)
+
+    V.wait_ge(S.ssq, 1)
+    A.wait_ge(S.ssq, 1)
+    for b in range(G):
+        if b < G // 2:
+            V.tensor_scalar(T.ht[:, b:TW:G], bank(b, NC), T.sv[:, b:b + 1], None, AluOpType.mult).then_inc(S.hd, 1)
+        else:
+            A.activation(T.ht[:, b:TW:G], bank(b, NC), AF.Copy, scale=T.sv[:, b:b + 1]).then_inc(S.hd, 1)
+    V.wait_ge(S.hd, G)
+    V.quantize_mx(T.hq[:, NC * r:NC * r + NC], T.hs[:, NC * r:NC * r + NC], T.ht[:]).then_inc(S.hqd, 1)
+    g.wait_ge(S.hqd, 1)
+    _send(g, topo, core, plane, plane, hcores, on, S.hcs, S.sent)
+    _send(g, topo, core, codes, codes, hcores, on, S.hcq, S.sent)
+    _send(g, topo, core, plane, plane, dcores, off, S["arr%d" % k], S.sent)
+    _send(g, topo, core, codes, codes, dcores, off, S["arr%d" % k], S.sent)
+    SY.wait_ge(S.hd, G)
+    SY.wait_ge(S.sent, _bits(hi) + 3 * _bits(off) + 2 * _bits(on))
+    SY.dma_start(T.h[:], T.ht[:]).then_inc(S.st, 16)
+
+    TE.wait_ge(S.qv, 1)
+    TE.wait_ge(S.hqd, 1)
+    for n, p in enumerate(P["order"][k]):
+        c0, c1 = 2 * NC * p, 2 * NC * p + 2 * NC
+        b = (G + n) % 8
+        TE.wait_ge(S["arr%d" % p], (1 if p == k else 2) * 2 * _bits(off))
+        TE.matmul_mx(bank(b, 2 * NC), T.w2q[:], T.w2s[:], T.hq[:, c0:c1], T.hs[:, c0:c1], True, True).then_inc(S["ym%d" % p], 1)
+        if n % 2 == 0:
+            V.wait_ge(S["ym%d" % p], 1)
+            V.tensor_copy(T.ys[:, c0:c1], bank(b, 2 * NC)).then_inc(S["yc%d" % p], 1)
+        else:
+            A.wait_ge(S["ym%d" % p], 1)
+            A.activation(T.ys[:, c0:c1], bank(b, 2 * NC), AF.Copy).then_inc(S["yc%d" % p], 1)
+        SY.wait_ge(S["yc%d" % p], 1)
+        SY.dma_start(T.y[:, c0:c1], T.ys[:, c0:c1]).then_inc(S.st, 16)
+    SY.wait_ge(S.st, 16 * (NP + 1))
+
+
+def rank_program(g, core, T, topo):
+    P = _plan(T, topo)
+    r = T.rank_of(core)
+    if r is not None:
+        _rank(g, core, r, T, topo, P)
+    elif core in P["job"]:
+        _helper(g, core, T, topo, P)

@@ -5,6 +5,7 @@ N, NP, NC, G, EPS = 12, 6, 128, 4, 0.001
 NSIM = 256
 TW = 4 * NC
 BANK = 512
+NY = NP + 1
 
 SCRATCH = {
     "xt": ("sbuf", [128, TW], "bfloat16"),
@@ -22,9 +23,10 @@ SCRATCH = {
     "hq": ("sbuf", [128, N * NC], "float8_e4m3fn_x4"), "hs": ("sbuf", [128, N * NC], "uint8"),
     "ys": ("sbuf", [128, N * NC], "float32"),
 }
-SEMAPHORES = (["ldx", "ldv", "qx", "qv", "ssd", "ssarr", "red", "va", "vr", "ssq", "hd", "hqd", "st", "sent", "hss", "hcq", "hcs"]
+SEMAPHORES = (["ldx", "ldv", "qx", "qv", "ssd0", "ssd", "ssarr0", "ssarr", "ssarrd", "red0", "vr0", "ssq0", "red", "va", "vr", "ssq",
+               "hd", "hqd", "st", "sent", "hss0", "hss", "hcq", "hcs"]
               + ["ldw%d" % i for i in range(G)] + ["qw%d" % i for i in range(G)] + ["mm%d" % i for i in range(G)]
-              + ["arr%d" % k for k in range(NP)] + ["ym%d" % k for k in range(NP)] + ["yc%d" % k for k in range(NP)])
+              + ["arr%d" % k for k in range(NP)] + ["ym%d" % k for k in range(NY)] + ["yc%d" % k for k in range(NY)])
 
 
 def _bits(mask):
@@ -79,20 +81,21 @@ def _plan(T, topo):
     return {"cores": cores, "direct": direct, "helpers": helpers, "job": job, "order": order}
 
 
-def _send(g, topo, core, view_src, view_dst, dests, mask, rsem, lsem):
+def _send(g, topo, core, view, dests, mask, rsem, lsem):
     ids = []
     for d in dests:
         rid, pid = topo.addr(d, core)
         ids.append(DstId(rid=rid, pnc=pid))
     g.remote_dma_fused([RemoteDMATransfer(dst_ids=ids, dma_engine_mask=mask, remote_sem=rsem,
-                                          srcs=[view_src], dsts=[view_dst] * len(dests))], local_sem=lsem)
+                                          srcs=[view], dsts=[view] * len(dests))], local_sem=lsem)
 
 
 def _views(T, r):
-    ss = T.land[:, G * r:G * r + G]
+    first = T.land[:, G * r:G * r + 1]
+    rest = T.land[:, G * r + 1:G * r + G]
     codes = T.hq[:, NC * r:NC * r + NC].bitcast(dt.uint8)
     plane = T.hs[:, NC * r:NC * r + NC]
-    return ss, codes, plane
+    return first, rest, codes, plane
 
 
 def _common(topo, core, dests):
@@ -110,15 +113,17 @@ def _helper(g, core, T, topo, P):
     on = _common(topo, rc, [h for h, _ in P["helpers"][r]])
     hi = on & ~_common(topo, rc, [P["cores"][r ^ 1]])
     m = _common(topo, core, dests)
-    ss, codes, plane = _views(T, r)
+    first, rest, codes, plane = _views(T, r)
     arr = S["arr%d" % (r // 2)]
+    g.wait_ge(S.hss0, _bits(hi))
+    _send(g, topo, core, first, dests, m, S.ssarr0, S.sent)
     g.wait_ge(S.hss, _bits(hi))
-    _send(g, topo, core, ss, ss, dests, m, S.ssarr, S.sent)
-    g.wait_ge(S.hcs, _bits(on))
-    _send(g, topo, core, plane, plane, dests, m, arr, S.sent)
+    _send(g, topo, core, rest, dests, m, S.ssarr, S.sent)
     g.wait_ge(S.hcq, _bits(on))
-    _send(g, topo, core, codes, codes, dests, m, arr, S.sent)
-    g.wait_ge(S.sent, 3 * _bits(m))
+    _send(g, topo, core, codes, dests, m, arr, S.sent)
+    g.wait_ge(S.hcs, _bits(on))
+    _send(g, topo, core, plane, dests, m, arr, S.sent)
+    g.wait_ge(S.sent, 4 * _bits(m))
 
 
 def _rank(g, core, r, T, topo, P):
@@ -132,7 +137,8 @@ def _rank(g, core, r, T, topo, P):
     on = _common(topo, core, hcores)
     off = _common(topo, core, dcores)
     hi = on & ~off
-    ss, codes, plane = _views(T, r)
+    first, rest, codes, plane = _views(T, r)
+    mean = 1.0 / (N * NC)
 
     def bank(b, n):
         return T.ps[:, BANK * b:BANK * b + n]
@@ -153,57 +159,71 @@ def _rank(g, core, r, T, topo, P):
         TE.matmul_mx(bank(i, NC), T.w1q[:, c0:c1], T.w1s[:, c0:c1], T.xq[:], T.xs[:], True, True).then_inc(S["mm%d" % i], 1)
         A.wait_ge(S["mm%d" % i], 1)
         A.activation(T.sq[:, c0:c1], bank(i, NC), AF.Square,
-                     accum_out=T.land[:, G * r + i:G * r + i + 1]).then_inc(S.ssd, 1)
+                     accum_out=T.land[:, G * r + i:G * r + i + 1]).then_inc(S.ssd0 if i == 0 else S.ssd, 1)
     V.wait_ge(S.ldv, 16)
     V.quantize_mx(T.w2q[:], T.w2s[:], T.w2t[:]).then_inc(S.qv, 1)
 
-    g.wait_ge(S.ssd, G)
-    _send(g, topo, core, ss, ss, hcores, hi, S.hss, S.sent)
-    _send(g, topo, core, ss, ss, dcores, off, S.ssarr, S.sent)
-    V.wait_ge(S.ssd, G)
-    V.wait_ge(S.ssarr, (N - 1) * _bits(off))
-    for i in range(G):
+    g.wait_ge(S.ssd0, 1)
+    _send(g, topo, core, first, hcores, hi, S.hss0, S.sent)
+    g.wait_ge(S.ssd, G - 1)
+    _send(g, topo, core, rest, hcores, hi, S.hss, S.sent)
+    _send(g, topo, core, T.land[:, G * r:G * r + G], dcores, off, S.ssarrd, S.sent)
+    far = (N - 1 - len(dcores)) * _bits(off)
+    V.wait_ge(S.ssd0, 1)
+    V.wait_ge(S.ssarrd, len(dcores) * _bits(off))
+    V.wait_ge(S.ssarr0, far)
+    V.tensor_reduce(T.tot[:, 0:1], T.land[:, 0:G * N:G], AxisListType.X, AluOpType.add).then_inc(S.red0, 1)
+    A.wait_ge(S.red0, 1)
+    A.activation(T.av[:, 0:1], T.tot[:, 0:1], AF.Sqrt, bias=EPS, scale=mean).then_inc(S.ssq0, 1)
+    V.wait_ge(S.ssd, G - 1)
+    V.wait_ge(S.ssarr, far)
+    for i in range(1, G):
         V.tensor_reduce(T.tot[:, i:i + 1], T.land[:, i:G * N:G], AxisListType.X, AluOpType.add).then_inc(S.red, 1)
-    V.wait_ge(S.red, G)
-    V.tensor_scalar(T.av[:], T.tot[:], 1.0 / (N * NC), EPS, AluOpType.mult, AluOpType.add).then_inc(S.va, 1)
+    V.wait_ge(S.red, G - 1)
+    V.tensor_scalar(T.av[:, 1:G], T.tot[:, 1:G], mean, EPS, AluOpType.mult, AluOpType.add).then_inc(S.va, 1)
     V.wait_ge(S.va, 1)
-    V.reciprocal(T.rc[:], T.av[:]).then_inc(S.vr, 1)
+    V.reciprocal(T.rc[:, 1:G], T.av[:, 1:G]).then_inc(S.vr, 1)
     A.wait_ge(S.vr, 1)
-    A.activation(T.sv[:], T.rc[:], AF.Sqrt).then_inc(S.ssq, 1)
+    A.activation(T.sv[:, 1:G], T.rc[:, 1:G], AF.Sqrt).then_inc(S.ssq, 1)
 
-    V.wait_ge(S.ssq, 1)
+    V.wait_ge(S.ssq0, 1)
+    V.reciprocal(T.sv[:, 0:1], T.av[:, 0:1]).then_inc(S.vr0, 1)
+    V.wait_ge(S.vr0, 1)
+    V.tensor_scalar(T.ht[:, 0:TW:G], bank(0, NC), T.sv[:, 0:1], None, AluOpType.mult).then_inc(S.hd, 1)
     A.wait_ge(S.ssq, 1)
-    for b in range(G):
-        if b < G // 2:
-            V.tensor_scalar(T.ht[:, b:TW:G], bank(b, NC), T.sv[:, b:b + 1], None, AluOpType.mult).then_inc(S.hd, 1)
-        else:
-            A.activation(T.ht[:, b:TW:G], bank(b, NC), AF.Copy, scale=T.sv[:, b:b + 1]).then_inc(S.hd, 1)
+    for b in range(1, G):
+        A.activation(T.ht[:, b:TW:G], bank(b, NC), AF.Copy, scale=T.sv[:, b:b + 1]).then_inc(S.hd, 1)
     V.wait_ge(S.hd, G)
     V.quantize_mx(T.hq[:, NC * r:NC * r + NC], T.hs[:, NC * r:NC * r + NC], T.ht[:]).then_inc(S.hqd, 1)
     g.wait_ge(S.hqd, 1)
-    _send(g, topo, core, plane, plane, hcores, on, S.hcs, S.sent)
-    _send(g, topo, core, codes, codes, hcores, on, S.hcq, S.sent)
-    _send(g, topo, core, plane, plane, dcores, off, S["arr%d" % k], S.sent)
-    _send(g, topo, core, codes, codes, dcores, off, S["arr%d" % k], S.sent)
+    _send(g, topo, core, codes, hcores, on, S.hcq, S.sent)
+    _send(g, topo, core, plane, hcores, on, S.hcs, S.sent)
+    _send(g, topo, core, plane, dcores, off, S["arr%d" % k], S.sent)
+    _send(g, topo, core, codes, dcores, off, S["arr%d" % k], S.sent)
     SY.wait_ge(S.hd, G)
-    SY.wait_ge(S.sent, _bits(hi) + 3 * _bits(off) + 2 * _bits(on))
+    SY.wait_ge(S.sent, 2 * _bits(hi) + 3 * _bits(off) + 2 * _bits(on))
     SY.dma_start(T.h[:], T.ht[:]).then_inc(S.st, 16)
 
     TE.wait_ge(S.qv, 1)
     TE.wait_ge(S.hqd, 1)
-    for n, p in enumerate(P["order"][k]):
-        c0, c1 = 2 * NC * p, 2 * NC * p + 2 * NC
-        b = (G + n) % 8
+    n = 0
+    for pos, p in enumerate(P["order"][k]):
         TE.wait_ge(S["arr%d" % p], (1 if p == k else 2) * 2 * _bits(off))
-        TE.matmul_mx(bank(b, 2 * NC), T.w2q[:], T.w2s[:], T.hq[:, c0:c1], T.hs[:, c0:c1], True, True).then_inc(S["ym%d" % p], 1)
-        if n % 2 == 0:
-            V.wait_ge(S["ym%d" % p], 1)
-            V.tensor_copy(T.ys[:, c0:c1], bank(b, 2 * NC)).then_inc(S["yc%d" % p], 1)
-        else:
-            A.wait_ge(S["ym%d" % p], 1)
-            A.activation(T.ys[:, c0:c1], bank(b, 2 * NC), AF.Copy).then_inc(S["yc%d" % p], 1)
-        SY.wait_ge(S["yc%d" % p], 1)
-        SY.dma_start(T.y[:, c0:c1], T.ys[:, c0:c1]).then_inc(S.st, 16)
+        parts = 2 if pos == NP - 1 else 1
+        cols = 2 * NC // parts
+        for t in range(parts):
+            c0, b = 2 * NC * p + cols * t, (G + n) % 8
+            c1 = c0 + cols
+            TE.matmul_mx(bank(b, cols), T.w2q[:], T.w2s[:], T.hq[:, c0:c1], T.hs[:, c0:c1], True, True).then_inc(S["ym%d" % n], 1)
+            if n % 2 == 0:
+                V.wait_ge(S["ym%d" % n], 1)
+                V.tensor_copy(T.ys[:, c0:c1], bank(b, cols)).then_inc(S["yc%d" % n], 1)
+            else:
+                A.wait_ge(S["ym%d" % n], 1)
+                A.activation(T.ys[:, c0:c1], bank(b, cols), AF.Copy).then_inc(S["yc%d" % n], 1)
+            SY.wait_ge(S["yc%d" % n], 1)
+            n += 1
+        SY.dma_start(T.y[:, 2 * NC * p:2 * NC * p + 2 * NC], T.ys[:, 2 * NC * p:2 * NC * p + 2 * NC]).then_inc(S.st, 16)
     SY.wait_ge(S.st, 16 * (NP + 1))
 
 

from concourse.bass import DstId, RemoteDMATransfer
from concourse.mybir import dt, AluOpType, AxisListType, ActivationFunctionType

N, NP, NC, G, EPS = 12, 6, 128, 4, 0.001
NSIM = 256
TW = 4 * NC
BANK = 512
NY = NP + 1

SCRATCH = {
    "xt": ("sbuf", [128, TW], "bfloat16"),
    "w1t": ("sbuf", [128, G * TW], "bfloat16"),
    "w2t": ("sbuf", [128, TW], "bfloat16"),
    "xq": ("sbuf", [128, NC], "float8_e4m3fn_x4"), "xs": ("sbuf", [128, NC], "uint8"),
    "w1q": ("sbuf", [128, G * NC], "float8_e4m3fn_x4"), "w1s": ("sbuf", [128, G * NC], "uint8"),
    "w2q": ("sbuf", [128, NC], "float8_e4m3fn_x4"), "w2s": ("sbuf", [128, NC], "uint8"),
    "ps": ("psum", [128, 8 * BANK], "float32"),
    "sq": ("sbuf", [128, G * NC], "float32"),
    "land": ("sbuf", [128, G * N], "float32"),
    "tot": ("sbuf", [128, G], "float32"), "av": ("sbuf", [128, G], "float32"),
    "rc": ("sbuf", [128, G], "float32"), "sv": ("sbuf", [128, G], "float32"),
    "ht": ("sbuf", [128, TW], "bfloat16"),
    "hq": ("sbuf", [128, N * NC], "float8_e4m3fn_x4"), "hs": ("sbuf", [128, N * NC], "uint8"),
    "ys": ("sbuf", [128, N * NC], "float32"),
}
SEMAPHORES = (["ldx", "ldv", "qx", "qv", "ssd0", "ssd", "ssarr0", "ssarr", "ssarrd", "red0", "vr0", "ssq0", "red", "va", "vr", "ssq",
               "hd", "hqd", "st", "sent", "hss0", "hss", "hcq", "hcs"]
              + ["ldw%d" % i for i in range(G)] + ["qw%d" % i for i in range(G)] + ["mm%d" % i for i in range(G)]
              + ["arr%d" % k for k in range(NP)] + ["ym%d" % k for k in range(NY)] + ["yc%d" % k for k in range(NY)])


def _bits(mask):
    return bin(mask).count("1")


def _plan(T, topo):
    cores = list(T.cores)
    lead = [cores[2 * k] for k in range(NP)]
    planes = []
    for k in range(NP):
        for p in planes:
            if topo.same_plane(lead[p[0]], lead[k]):
                p.append(k)
                break
        else:
            planes.append([k])
    planes.sort(key=len)
    small, big = planes
    direct, route = {}, {}
    for i, k in enumerate(small):
        direct[k] = small[1 - i]
        route[k] = [None] * 4
        for j, o in enumerate(big):
            route[k][(j + 2 * i) % 4] = (o, j // 2 == i)
    for j, k in enumerate(big):
        direct[k] = big[(j + 1) % 4]
        route[k] = [None] * 4
        route[k][(j + 3) % 4] = (big[(j + 2) % 4], False)
        route[k][(j + 2) % 4] = (big[(j + 3) % 4], False)
        route[k][j % 4] = (small[0], j == 0)
        route[k][(j + 1) % 4] = (small[1], j == 1)
    helpers, job = {}, {}
    for r in range(N):
        rc, k, a = cores[r], r // 2, r % 2
        chipc = [c for c in range(NSIM) if c != rc and topo.host(c) == topo.host(rc) and topo.chip(c) == topo.chip(rc)]
        reach = {c: sum(1 for d in cores if topo.may_write(c, d)) for c in chipc}
        used, helpers[r] = [], []
        for o, near in route[k]:
            dests = [2 * o + a, 2 * o + 1 - a]
            cand = [c for c in chipc if c not in used and (topo.die(c) == topo.die(rc)) == near
                    and all(topo.may_write(c, cores[d]) for d in dests)]
            cand.sort(key=lambda c: (reach[c], c))
            used.append(cand[0])
            helpers[r].append((cand[0], dests))
            job[cand[0]] = (r, dests)
    order = {}
    for k in range(NP):
        order[k] = [k] + [p for p in range(NP) if direct[p] == k]
        for pos in range(4):
            order[k] += [p for p in range(NP) if p != k and route[p][pos][0] == k]
    return {"cores": cores, "direct": direct, "helpers": helpers, "job": job, "order": order}


def _send(g, topo, core, view, dests, mask, rsem, lsem):
    ids = []
    for d in dests:
        rid, pid = topo.addr(d, core)
        ids.append(DstId(rid=rid, pnc=pid))
    g.remote_dma_fused([RemoteDMATransfer(dst_ids=ids, dma_engine_mask=mask, remote_sem=rsem,
                                          srcs=[view], dsts=[view] * len(dests))], local_sem=lsem)


def _views(T, r):
    first = T.land[:, G * r:G * r + 1]
    rest = T.land[:, G * r + 1:G * r + G]
    codes = T.hq[:, NC * r:NC * r + NC].bitcast(dt.uint8)
    plane = T.hs[:, NC * r:NC * r + NC]
    return first, rest, codes, plane


def _common(topo, core, dests):
    m = topo.mask(core, dests[0])
    for d in dests[1:]:
        m &= topo.mask(core, d)
    return m


def _helper(g, core, T, topo, P):
    r, ranks = P["job"][core]
    S = T.sem
    dests = [P["cores"][d] for d in ranks]
    rc = P["cores"][r]
    on = _common(topo, rc, [h for h, _ in P["helpers"][r]])
    hi = on & ~_common(topo, rc, [P["cores"][r ^ 1]])
    m = _common(topo, core, dests)
    first, rest, codes, plane = _views(T, r)
    arr = S["arr%d" % (r // 2)]
    g.wait_ge(S.hss0, _bits(hi))
    _send(g, topo, core, first, dests, m, S.ssarr0, S.sent)
    g.wait_ge(S.hss, _bits(hi))
    _send(g, topo, core, rest, dests, m, S.ssarr, S.sent)
    g.wait_ge(S.hcq, _bits(on))
    _send(g, topo, core, codes, dests, m, arr, S.sent)
    g.wait_ge(S.hcs, _bits(on))
    _send(g, topo, core, plane, dests, m, arr, S.sent)
    g.wait_ge(S.sent, 4 * _bits(m))


def _rank(g, core, r, T, topo, P):
    S, cores = T.sem, P["cores"]
    k, a = r // 2, r % 2
    V, A, TE, SY = g.vector, g.scalar, g.tensor, g.sync
    AF = ActivationFunctionType
    hcores = [h for h, _ in P["helpers"][r]]
    o = P["direct"][k]
    dcores = [cores[r ^ 1], cores[2 * o + a], cores[2 * o + 1 - a]]
    on = _common(topo, core, hcores)
    off = _common(topo, core, dcores)
    hi = on & ~off
    first, rest, codes, plane = _views(T, r)
    mean = 1.0 / (N * NC)

    def bank(b, n):
        return T.ps[:, BANK * b:BANK * b + n]

    SY.dma_start(T.xt[:], T.x[:]).then_inc(S.ldx, 16)
    for i in range(G):
        q = A if i % 2 == 0 else SY
        q.dma_start(T.w1t[:, TW * i:TW * i + TW], T.w1[:, TW * i:TW * i + TW]).then_inc(S["ldw%d" % i], 16)
    SY.dma_start(T.w2t[:], T.w2[:]).then_inc(S.ldv, 16)
    V.wait_ge(S.ldx, 16)
    V.quantize_mx(T.xq[:], T.xs[:], T.xt[:]).then_inc(S.qx, 1)
    TE.wait_ge(S.qx, 1)
    for i in range(G):
        c0, c1 = NC * i, NC * i + NC
        V.wait_ge(S["ldw%d" % i], 16)
        V.quantize_mx(T.w1q[:, c0:c1], T.w1s[:, c0:c1], T.w1t[:, TW * i:TW * i + TW]).then_inc(S["qw%d" % i], 1)
        TE.wait_ge(S["qw%d" % i], 1)
        TE.matmul_mx(bank(i, NC), T.w1q[:, c0:c1], T.w1s[:, c0:c1], T.xq[:], T.xs[:], True, True).then_inc(S["mm%d" % i], 1)
        A.wait_ge(S["mm%d" % i], 1)
        A.activation(T.sq[:, c0:c1], bank(i, NC), AF.Square,
                     accum_out=T.land[:, G * r + i:G * r + i + 1]).then_inc(S.ssd0 if i == 0 else S.ssd, 1)
    V.wait_ge(S.ldv, 16)
    V.quantize_mx(T.w2q[:], T.w2s[:], T.w2t[:]).then_inc(S.qv, 1)

    g.wait_ge(S.ssd0, 1)
    _send(g, topo, core, first, hcores, hi, S.hss0, S.sent)
    g.wait_ge(S.ssd, G - 1)
    _send(g, topo, core, rest, hcores, hi, S.hss, S.sent)
    _send(g, topo, core, T.land[:, G * r:G * r + G], dcores, off, S.ssarrd, S.sent)
    far = (N - 1 - len(dcores)) * _bits(off)
    V.wait_ge(S.ssd0, 1)
    V.wait_ge(S.ssarrd, len(dcores) * _bits(off))
    V.wait_ge(S.ssarr0, far)
    V.tensor_reduce(T.tot[:, 0:1], T.land[:, 0:G * N:G], AxisListType.X, AluOpType.add).then_inc(S.red0, 1)
    A.wait_ge(S.red0, 1)
    A.activation(T.av[:, 0:1], T.tot[:, 0:1], AF.Sqrt, bias=EPS, scale=mean).then_inc(S.ssq0, 1)
    V.wait_ge(S.ssd, G - 1)
    V.wait_ge(S.ssarr, far)
    for i in range(1, G):
        V.tensor_reduce(T.tot[:, i:i + 1], T.land[:, i:G * N:G], AxisListType.X, AluOpType.add).then_inc(S.red, 1)
    V.wait_ge(S.red, G - 1)
    V.tensor_scalar(T.av[:, 1:G], T.tot[:, 1:G], mean, EPS, AluOpType.mult, AluOpType.add).then_inc(S.va, 1)
    V.wait_ge(S.va, 1)
    V.reciprocal(T.rc[:, 1:G], T.av[:, 1:G]).then_inc(S.vr, 1)
    A.wait_ge(S.vr, 1)
    A.activation(T.sv[:, 1:G], T.rc[:, 1:G], AF.Sqrt).then_inc(S.ssq, 1)

    V.wait_ge(S.ssq0, 1)
    V.reciprocal(T.sv[:, 0:1], T.av[:, 0:1]).then_inc(S.vr0, 1)
    V.wait_ge(S.vr0, 1)
    V.tensor_scalar(T.ht[:, 0:TW:G], bank(0, NC), T.sv[:, 0:1], None, AluOpType.mult).then_inc(S.hd, 1)
    A.wait_ge(S.ssq, 1)
    for b in range(1, G):
        A.activation(T.ht[:, b:TW:G], bank(b, NC), AF.Copy, scale=T.sv[:, b:b + 1]).then_inc(S.hd, 1)
    V.wait_ge(S.hd, G)
    V.quantize_mx(T.hq[:, NC * r:NC * r + NC], T.hs[:, NC * r:NC * r + NC], T.ht[:]).then_inc(S.hqd, 1)
    g.wait_ge(S.hqd, 1)
    _send(g, topo, core, codes, hcores, on, S.hcq, S.sent)
    _send(g, topo, core, plane, hcores, on, S.hcs, S.sent)
    _send(g, topo, core, plane, dcores, off, S["arr%d" % k], S.sent)
    _send(g, topo, core, codes, dcores, off, S["arr%d" % k], S.sent)
    SY.wait_ge(S.hd, G)
    SY.wait_ge(S.sent, 2 * _bits(hi) + 3 * _bits(off) + 2 * _bits(on))
    SY.dma_start(T.h[:], T.ht[:]).then_inc(S.st, 16)

    TE.wait_ge(S.qv, 1)
    TE.wait_ge(S.hqd, 1)
    n = 0
    for pos, p in enumerate(P["order"][k]):
        TE.wait_ge(S["arr%d" % p], (1 if p == k else 2) * 2 * _bits(off))
        parts = 2 if pos == NP - 1 else 1
        cols = 2 * NC // parts
        for t in range(parts):
            c0, b = 2 * NC * p + cols * t, (G + n) % 8
            c1 = c0 + cols
            TE.matmul_mx(bank(b, cols), T.w2q[:], T.w2s[:], T.hq[:, c0:c1], T.hs[:, c0:c1], True, True).then_inc(S["ym%d" % n], 1)
            if n % 2 == 0:
                V.wait_ge(S["ym%d" % n], 1)
                V.tensor_copy(T.ys[:, c0:c1], bank(b, cols)).then_inc(S["yc%d" % n], 1)
            else:
                A.wait_ge(S["ym%d" % n], 1)
                A.activation(T.ys[:, c0:c1], bank(b, cols), AF.Copy).then_inc(S["yc%d" % n], 1)
            SY.wait_ge(S["yc%d" % n], 1)
            n += 1
        SY.dma_start(T.y[:, 2 * NC * p:2 * NC * p + 2 * NC], T.ys[:, 2 * NC * p:2 * NC * p + 2 * NC]).then_inc(S.st, 16)
    SY.wait_ge(S.st, 16 * (NP + 1))


def rank_program(g, core, T, topo):
    P = _plan(T, topo)
    r = T.rank_of(core)
    if r is not None:
        _rank(g, core, r, T, topo, P)
    elif core in P["job"]:
        _helper(g, core, T, topo, P)
